import numpy as np
import ml_dtypes


def mxq(x, axis, fmt="e4m3"):
    dtype, down = {"e4m3": (ml_dtypes.float8_e4m3fn, 7), "e5m2": (ml_dtypes.float8_e5m2, 14)}[fmt]
    v = np.moveaxis(np.asarray(x, np.float32).astype(ml_dtypes.bfloat16).astype(np.float64), axis, -1)
    blocks = v.reshape(v.shape[:-1] + (-1, 32))
    amax = np.abs(blocks).max(-1, keepdims=True)
    byte = np.maximum(np.where(amax > 0, np.frexp(amax)[1] - 1 + 127, 0) - down, 1)
    scale = np.exp2(byte - 127.0)
    codes = (blocks / scale).astype(np.float32).astype(dtype).astype(np.float64)
    return np.moveaxis((codes * scale).reshape(v.shape), -1, axis)


WIDE = False


def mx_kscale(k):
    if not WIDE:
        return np.ones(k)
    levels = np.array([10, -10, 5, -5, 0])
    if k % 512:
        return np.exp2(np.random.permutation(np.resize(levels, k // 32))).repeat(32)
    a = np.empty((k // 512, 16))
    for p in range(k // 512):
        a[p, :8] = np.random.permutation(np.resize(levels, 8))
        for g in range(8):
            far = levels[np.abs(levels - a[p, g]) >= 10]
            a[p, g + 8] = far[np.random.randint(len(far))]
    return np.exp2(a.ravel()).repeat(32)


BF16 = ml_dtypes.bfloat16


def bf(x):
    return np.asarray(x, np.float32).astype(BF16)


def f64(x):
    return np.asarray(x).astype(np.float64)


E2M1 = np.array([0.0, 0.5, 1.0, 1.5, 2.0, 3.0, 4.0, 6.0, -0.0, -0.5, -1.0, -1.5, -2.0, -3.0, -4.0, -6.0])


def pack_weight(w, fmt):
    k, n = w.shape
    w = f64(bf(w)).reshape(k // 32, 32, n)
    amax = np.abs(w).max(1)
    if fmt == "e4m3":
        byte = np.frexp(amax)[1] - 1 + 127 - 7
    else:
        mant, ex = np.frexp(amax / 6.0)
        byte = np.where(mant > 0.5, ex, ex - 1) + 127
    byte = np.clip(np.where(amax > 0, byte, 1), 1, 254)
    scaled = (w * np.exp2(127.0 - byte)[:, None, :]).reshape(k, n).astype(np.float32)
    by_word = np.ascontiguousarray(scaled.reshape(k // 512, 128, 4, n).transpose(0, 1, 3, 2))
    if fmt == "e4m3":
        words = by_word.astype(ml_dtypes.float8_e4m3fn).view(np.uint8)
    else:
        c = by_word.astype(ml_dtypes.float4_e2m1fn).view(np.uint8) & 0xF
        words = c[..., 0::2] | (c[..., 1::2] << 4)
    return np.ascontiguousarray(words), np.ascontiguousarray(byte.astype(np.uint8).reshape(k // 512, 16, n))


def unpack_weight(words, scales, fmt):
    g, p, n, _ = words.shape
    if fmt == "e4m3":
        vals = np.ascontiguousarray(words).view(ml_dtypes.float8_e4m3fn).astype(np.float64)
    else:
        nib = np.empty((g, p, n, 4), np.uint8)
        nib[..., 0::2] = words & 0xF
        nib[..., 1::2] = words >> 4
        vals = E2M1[nib]
    vals = vals * np.repeat(np.exp2(scales.astype(np.float64) - 127.0), 8, axis=1)[..., None]
    return vals.transpose(0, 1, 3, 2).reshape(g * 512, n)
def pack4(w):
    words, scales = pack_weight(w, "e2m1")
    return words.reshape(words.shape[0], 128, -1), scales


def unpack4(words, scales):
    return unpack_weight(words.reshape(words.shape[0], 128, -1, 2), scales, "e2m1")


M, K, A, F, N = 2048, 512, 1024, 512, 512


def setup_inputs():
    s, r, t = mx_kscale(K), mx_kscale(F), mx_kscale(A)
    mix = np.random.lognormal(-1.5, 1.75, (K, M)) * s[:, None]
    atoms = np.random.lognormal(-1.125, 1.5, (K, A)) / K / s[:, None] * t
    own = np.random.lognormal(-0.8, 1.25, (A, F)) * np.random.lognormal(-0.3, 0.75, F)
    total = np.random.lognormal(-0.8, 1.25, (A, F)) * np.random.lognormal(-0.3, 0.75, F)
    split = np.concatenate([32.0 / A * own / t[:, None] ** 2, 8.0 / A * total / t[:, None]], axis=0)
    load = np.random.lognormal(-1.5, 1.75, (F, N))
    mix_words, mix_scales = pack4(mix)
    gain_words, gain_scales = pack4(atoms)
    return {"mix_words": mix_words, "mix_scales": mix_scales,
            "gain_words": gain_words, "gain_scales": gain_scales,
            "split": bf(split / np.sqrt(F) / r),
            "load": bf(load / np.sqrt(F) * r[:, None])}


def reference(mix_words, mix_scales, gain_words, gain_scales, split, load):
    c = unpack4(mix_words, mix_scales)
    d = unpack4(gain_words, gain_scales)
    beta = c.T @ d
    power = mxq(f64(split), 1, "e4m3") @ mxq(f64(load), 0, "e4m3")
    pq = mxq(power, 0, "e4m3")
    signal = mxq(beta * beta, 1, "e4m3") @ pq[:A]
    interference = mxq(beta, 1, "e4m3") @ pq[A:]
    return np.log(signal / interference)

@@ -1,0 +1,293 @@
+from contextlib import ExitStack
+
+import concourse.mybir as mybir
+from concourse.masks import make_identity
+
+M, K, A, F, N = 2048, 512, 1024, 512, 512
+
+F32 = mybir.dt.float32
+BF16 = mybir.dt.bfloat16
+I32 = mybir.dt.int32
+U32 = mybir.dt.uint32
+U8 = mybir.dt.uint8
+FP8X4 = mybir.dt.float8_e4m3fn_x4
+FP4X4 = mybir.dt.float4_e2m1fn_x4
+ACT = mybir.ActivationFunctionType
+ALU = mybir.AluOpType
+
+FLOPS = 2 * K * M * A + 2 * 2 * A * F * N + 2 * 2 * M * A * N
+BYTES = M * K // 2 + M * K // 32 + A * K // 2 + A * K // 32 + 2 * (2 * A * F + F * N) + 4 * M * N
+
+P = 128
+MT = M // P
+LEAD = 2
+
+
+def tile_cell_free_log_sir_s12_kernel(tc, mix_words, mix_scales, gain_words, gain_scales, split, load, out):
+    nc = tc.nc
+    with ExitStack() as ctx:
+        keep = ctx.enter_context(tc.tile_pool(name="keep", bufs=1))
+        work = ctx.enter_context(tc.tile_pool(name="work", bufs=4))
+        psum = ctx.enter_context(tc.psum_pool(name="psum", bufs=2))
+
+        mixw = keep.tile([P, 2 * M], U8, name="mixw", align_bytes=64)
+        mixs = keep.tile([P, M], U8, name="mixs", align_bytes=64)
+        graw = keep.tile([P, 2 * A], U8, name="graw", align_bytes=64)
+        gsraw = keep.tile([P, A], U8, name="gsraw", align_bytes=64)
+        gw = keep.tile([P, 2 * A], U8, name="gw", align_bytes=64)
+        gs = keep.tile([P, A], U8, name="gs", align_bytes=64)
+        ident = keep.tile([P, P], F32, name="ident", align_bytes=64)
+        sp = [keep.tile([P, 4 * F], BF16, name="sp%d" % k, align_bytes=64) for k in range(4)]
+        spg = [keep.tile([P, 4 * P, 4], BF16, name="spg%d" % k, align_bytes=64) for k in range(4)]
+        spc = [keep.tile([P, 4 * P], U32, name="spc%d" % k, align_bytes=64) for k in range(4)]
+        sps = [keep.tile([P, 4 * P], U8, name="sps%d" % k, align_bytes=64) for k in range(4)]
+        lraw = keep.tile([P, 4, N], BF16, name="lraw", align_bytes=64)
+        lg = keep.tile([P, N, 4], BF16, name="lg", align_bytes=64)
+        lc = keep.tile([P, N], U32, name="lc", align_bytes=64)
+        lsc = keep.tile([P, N], U8, name="lsc", align_bytes=64)
+        pw = [keep.tile([P, N, 4], BF16, name="pw%d" % k, align_bytes=64) for k in range(4)]
+        pc = [keep.tile([P, N], U32, name="pc%d" % k, align_bytes=64) for k in range(4)]
+        ps = [keep.tile([P, N], U8, name="ps%d" % k, align_bytes=64) for k in range(4)]
+        warm = keep.tile([P, 1], F32, name="warm")
+
+        mix_w = mix_words.rearrange("o p b -> (o p) b")
+        mix_s = mix_scales.rearrange("o q n -> (o q) n")
+        gain_w = gain_words.rearrange("o p b -> (o p) b")
+        gain_s = gain_scales.rearrange("o q n -> (o q) n")
+
+        ctx.enter_context(tc.manual_schedule())
+
+        nc.vector.memset(gsraw[:].bitcast(I32), 0)
+        nc.vector.memset(mixs[:].bitcast(I32), 0)
+        nc.vector.memset(warm[:], 1.0)
+        nc.scalar.activation(out=warm[:], in_=warm[:], func=ACT.Ln)
+        for r in range(4):
+            nc.sync.dma_start(out=gsraw[r:P:32, :].bitcast(I32), in_=gain_s[r:16:4, :].bitcast(I32))
+        nc.sync.dma_start(out=graw[:].bitcast(I32), in_=gain_w.bitcast(I32))
+        nc.sync.dma_start(out=mixw[:, 0:1024].bitcast(I32), in_=mix_w[:, 0:1024].bitcast(I32))
+        for r in range(4):
+            eng = nc.sync if r < 2 else nc.gpsimd
+            eng.dma_start(out=mixs[r:P:32, :].bitcast(I32), in_=mix_s[r:16:4, :].bitcast(I32))
+        make_identity(nc, ident[:])
+        nc.sync.dma_start(out=sp[0][:], in_=split[0:512, :].rearrange("(p s) f -> p (s f)", s=4))
+        nc.sync.dma_start(out=lraw[:], in_=load.rearrange("(p j) n -> p j n", j=4))
+        nc.sync.dma_start(out=sp[1][:], in_=split[512:1024, :].rearrange("(p s) f -> p (s f)", s=4))
+        nc.sync.dma_start(out=mixw[:, 1024:4096].bitcast(I32), in_=mix_w[:, 1024:4096].bitcast(I32))
+        for k in (2, 3):
+            nc.sync.dma_start(out=sp[k][:], in_=split[512 * k : 512 * (k + 1), :].rearrange("(p s) f -> p (s f)", s=4))
+
+        def permute(g):
+            nc.vector.tensor_copy(
+                out=gs[:, 512 * g : 512 * (g + 1)].rearrange("p (t x y) -> p t x y", t=4, y=2),
+                in_=gsraw[:, 512 * g : 512 * (g + 1)].rearrange("p (x t y) -> p t x y", t=4, y=2),
+            )
+            nc.vector.tensor_copy(
+                out=gw[:, 1024 * g : 1024 * (g + 1)].bitcast(I32).rearrange("p (t x) -> p t x", t=4),
+                in_=graw[:, 1024 * g : 1024 * (g + 1)].bitcast(I32).rearrange("p (x t) -> p t x", t=4),
+            )
+
+        wbank = {}
+        bt, bq = {}, {}
+
+        def beta_mm(m, g):
+            w = psum.tile([P, 4, P], F32, name="w", bufs=4)
+            wbank[(m, g)] = w
+            for t in range(4):
+                c = (4 * g + t) * P
+                nc.tensor.matmul_mx(
+                    out=w[:, t, :],
+                    lhsT=gw[:, 2 * c : 2 * (c + P)].bitcast(FP4X4),
+                    lhsT_scale=gs[:, c : c + P],
+                    rhs=mixw[:, 2 * m * P : 2 * (m + 1) * P].bitcast(FP4X4),
+                    rhs_scale=mixs[:, m * P : (m + 1) * P],
+                    start=(t == 0),
+                    stop=(t == 3),
+                )
+
+        def beta_copy(m, g):
+            if g == 0:
+                bt[m] = work.tile([P, 2, 2, P, 4], BF16, name="bt", align_bytes=64)
+            nc.vector.tensor_copy(out=bt[m][:, 1, g], in_=wbank[(m, g)][:].rearrange("p t u -> p u t"))
+
+        def beta_square(m, g):
+            nc.scalar.activation(out=bt[m][:, 0, g], in_=wbank[(m, g)][:].rearrange("p t u -> p u t"), func=ACT.Square)
+
+        def quant(dst_c, dst_s, src):
+            nc.vector.quantize_mx(out=dst_c.bitcast(FP8X4), scales=dst_s, in_=src)
+
+        def q_beta(m):
+            c = work.tile([P, 4 * P], U32, name="bc", align_bytes=64)
+            s = work.tile([P, 4 * P], U8, name="bs", align_bytes=64)
+            bq[m] = (c, s)
+            quant(c[:], s[:], bt[m][:].rearrange("p a g u t -> p (a g u t)"))
+
+        tbank = {}
+
+        def transposes(k):
+            words = sp[k][:].bitcast(F32)
+            for h in range(2):
+                if h == 0:
+                    b = psum.tile([P, 4, P], F32, name="sg", bufs=2)
+                else:
+                    b = psum.tile([P, 4, P], F32, name="it", bufs=2)
+                tbank[(k, h)] = b
+                for y in range(2):
+                    for u in range(2):
+                        o = (2 * h + y) * 256 + u
+                        nc.tensor.transpose(b[:, 2 * y + u, :], words[:, o : o + 255 : 2], ident[:])
+
+        def split_copy(k, h, eng):
+            dst = spg[k][:].rearrange("p c j -> p (c j)").bitcast(F32).rearrange("p (a h x v) -> p h a x v", a=2, h=2, v=4)[:, h]
+            src = tbank[(k, h)][:].rearrange("p v (x a) -> p a x v", a=2)
+            if eng == "s":
+                nc.scalar.copy(out=dst, in_=src)
+            else:
+                nc.vector.tensor_copy(out=dst, in_=src)
+
+        def q_split(k):
+            quant(spc[k][:], sps[k][:], spg[k][:].rearrange("p c j -> p (c j)"))
+
+        def load_copy(i):
+            c = slice(256 * i, 256 * (i + 1))
+            nc.gpsimd.tensor_scalar(
+                out=lg[:, c, :],
+                in0=lraw[:, :, c].rearrange("p t n -> p n t"),
+                scalar1=1.0,
+                scalar2=0.0,
+                op0=ALU.mult,
+                op1=ALU.add,
+            )
+
+        def q_load():
+            quant(lc[:], lsc[:], lg[:].rearrange("p n j -> p (n j)"))
+
+        pbank = {}
+
+        def power_mm(k, b):
+            w = psum.tile([P, 4, P], F32, name="w", bufs=4)
+            pbank[(k, b)] = w
+            for t in range(4):
+                nc.tensor.matmul_mx(
+                    out=w[:, t, :],
+                    lhsT=spc[k][:, t * P : (t + 1) * P].bitcast(FP8X4),
+                    lhsT_scale=sps[k][:, t * P : (t + 1) * P],
+                    rhs=lc[:, b * P : (b + 1) * P].bitcast(FP8X4),
+                    rhs_scale=lsc[:, b * P : (b + 1) * P],
+                    start=True,
+                    stop=True,
+                )
+
+        def power_copy(k, b, eng):
+            dst = pw[k][:, b * P : (b + 1) * P, :]
+            src = pbank[(k, b)][:].rearrange("p t n -> p n t")
+            if eng == "s":
+                nc.scalar.copy(out=dst, in_=src)
+            else:
+                nc.vector.tensor_copy(out=dst, in_=src)
+
+        def q_power(k):
+            quant(pc[k][:], ps[k][:], pw[k][:].rearrange("p n t -> p (n t)"))
+
+        sgb, itb, lns, lni = {}, {}, {}, {}
+
+        def stage2(m, which):
+            base = 0 if which == "sg" else 2
+            if which == "sg":
+                acc = psum.tile([P, N], F32, name="sg", bufs=2)
+                sgb[m] = acc
+            else:
+                acc = psum.tile([P, N], F32, name="it", bufs=2)
+                itb[m] = acc
+            for g in range(2):
+                nc.tensor.matmul_mx(
+                    out=acc[:],
+                    lhsT=bq[m][0][:, (base + g) * P : (base + g + 1) * P].bitcast(FP8X4),
+                    lhsT_scale=bq[m][1][:, (base + g) * P : (base + g + 1) * P],
+                    rhs=pc[base + g][:].bitcast(FP8X4),
+                    rhs_scale=ps[base + g][:],
+                    start=(g == 0),
+                    stop=(g == 1),
+                )
+
+        def log_int(m):
+            lni[m] = work.tile([P, N], F32, name="lni")
+            nc.scalar.activation(out=lni[m][:], in_=itb[m][:], func=ACT.Ln)
+
+        def log_sig(m):
+            lns[m] = work.tile([P, N], F32, name="lns")
+            nc.scalar.activation(out=lns[m][:], in_=sgb[m][:], func=ACT.Ln)
+
+        def finish(m):
+            res = work.tile([P, N], F32, name="res")
+            nc.vector.tensor_tensor(out=res[:], in0=lns[m][:], in1=lni[m][:], op=ALU.subtract)
+            nc.sync.dma_start(out=out[m * P : (m + 1) * P, :], in_=res[:])
+
+        permute(0)
+        beta_mm(0, 0)
+        permute(1)
+        beta_mm(0, 1)
+        beta_mm(1, 0)
+        beta_mm(1, 1)
+        load_copy(0)
+        load_copy(1)
+        for m in (0, 1):
+            for g in range(2):
+                beta_copy(m, g)
+                beta_square(m, g)
+        transposes(0)
+        beta_mm(2, 0)
+        beta_mm(2, 1)
+        transposes(1)
+        split_copy(0, 0, "s")
+        split_copy(0, 1, "v")
+        q_beta(0)
+        q_load()
+        q_split(0)
+        for b in range(4):
+            power_mm(0, b)
+        beta_copy(2, 0)
+        beta_square(2, 0)
+        beta_copy(2, 1)
+        beta_square(2, 1)
+        split_copy(1, 0, "s")
+        split_copy(1, 1, "s")
+        q_beta(1)
+        q_split(1)
+        transposes(2)
+        for k in range(4):
+            for b in range(4):
+                power_copy(k, b, "v" if b == 3 else "s")
+            if k + 1 < 4:
+                for b in range(4):
+                    power_mm(k + 1, b)
+            if k + 2 < 4:
+                split_copy(k + 2, 0, "s")
+                split_copy(k + 2, 1, "s")
+            if k + 3 < 4:
+                transposes(k + 3)
+            if k == 0:
+                q_beta(2)
+            q_power(k)
+            if k + 2 < 4:
+                q_split(k + 2)
+
+        for i in range(MT):
+            j = i + LEAD
+            beta = 2 < j < MT
+            stage2(i, "it")
+            stage2(i, "sg")
+            if beta:
+                beta_mm(j, 0)
+                beta_mm(j, 1)
+                beta_copy(j, 0)
+                beta_square(j, 0)
+                beta_square(j, 1)
+            if 2 < j - 1 < MT:
+                q_beta(j - 1)
+            if beta:
+                beta_copy(j, 1)
+            if i > 0:
+                finish(i - 1)
+            log_int(i)
+            log_sig(i)
+        finish(MT - 1)

@@ -61,20 +61,26 @@ def tile_cell_free_log_sir_s12_kernel(tc, mix_words, mix_scales, gain_words, gai
         nc.vector.memset(mixs[:].bitcast(I32), 0)
         nc.vector.memset(warm[:], 1.0)
         nc.scalar.activation(out=warm[:], in_=warm[:], func=ACT.Ln)
+        make_identity(nc, ident[:])
+
+        def load_split(k):
+            nc.sync.dma_start(out=sp[k][:], in_=split[512 * k : 512 * (k + 1), :].rearrange("(p s) f -> p (s f)", s=4))
+
+        def load_mix(a, b):
+            nc.sync.dma_start(out=mixw[:, a:b].bitcast(I32), in_=mix_w[:, a:b].bitcast(I32))
+
+        load_split(0)
+        nc.sync.dma_start(out=graw[:].bitcast(I32), in_=gain_w.bitcast(I32))
         for r in range(4):
             nc.sync.dma_start(out=gsraw[r:P:32, :].bitcast(I32), in_=gain_s[r:16:4, :].bitcast(I32))
-        nc.sync.dma_start(out=graw[:].bitcast(I32), in_=gain_w.bitcast(I32))
-        nc.sync.dma_start(out=mixw[:, 0:1024].bitcast(I32), in_=mix_w[:, 0:1024].bitcast(I32))
+        load_mix(0, 1024)
         for r in range(4):
-            eng = nc.sync if r < 2 else nc.gpsimd
-            eng.dma_start(out=mixs[r:P:32, :].bitcast(I32), in_=mix_s[r:16:4, :].bitcast(I32))
-        make_identity(nc, ident[:])
-        nc.sync.dma_start(out=sp[0][:], in_=split[0:512, :].rearrange("(p s) f -> p (s f)", s=4))
+            nc.sync.dma_start(out=mixs[r:P:32, :].bitcast(I32), in_=mix_s[r:16:4, :].bitcast(I32))
         nc.sync.dma_start(out=lraw[:], in_=load.rearrange("(p j) n -> p j n", j=4))
-        nc.sync.dma_start(out=sp[1][:], in_=split[512:1024, :].rearrange("(p s) f -> p (s f)", s=4))
-        nc.sync.dma_start(out=mixw[:, 1024:4096].bitcast(I32), in_=mix_w[:, 1024:4096].bitcast(I32))
-        for k in (2, 3):
-            nc.sync.dma_start(out=sp[k][:], in_=split[512 * k : 512 * (k + 1), :].rearrange("(p s) f -> p (s f)", s=4))
+        load_split(1)
+        load_mix(1024, 4096)
+        load_split(2)
+        load_split(3)
 
         def permute(g):
             nc.vector.tensor_copy(
@@ -90,6 +96,8 @@ def tile_cell_free_log_sir_s12_kernel(tc, mix_words, mix_scales, gain_words, gai
         bt, bq = {}, {}
 
         def beta_mm(m, g):
+            if g == 0:
+                bt[m] = work.tile([P, 2, 2, P, 4], BF16, name="bt", align_bytes=64)
             w = psum.tile([P, 4, P], F32, name="w", bufs=4)
             wbank[(m, g)] = w
             for t in range(4):
@@ -105,8 +113,6 @@ def tile_cell_free_log_sir_s12_kernel(tc, mix_words, mix_scales, gain_words, gai
                 )
 
         def beta_copy(m, g):
-            if g == 0:
-                bt[m] = work.tile([P, 2, 2, P, 4], BF16, name="bt", align_bytes=64)
             nc.vector.tensor_copy(out=bt[m][:, 1, g], in_=wbank[(m, g)][:].rearrange("p t u -> p u t"))
 
         def beta_square(m, g):
@@ -222,66 +228,84 @@ def tile_cell_free_log_sir_s12_kernel(tc, mix_words, mix_scales, gain_words, gai
             nc.vector.tensor_tensor(out=res[:], in0=lns[m][:], in1=lni[m][:], op=ALU.subtract)
             nc.sync.dma_start(out=out[m * P : (m + 1) * P, :], in_=res[:])
 
+        transposes(0)
         permute(0)
-        beta_mm(0, 0)
         permute(1)
-        beta_mm(0, 1)
-        beta_mm(1, 0)
-        beta_mm(1, 1)
-        load_copy(0)
-        load_copy(1)
+        split_copy(0, 0, "s")
+        split_copy(0, 1, "s")
         for m in (0, 1):
             for g in range(2):
-                beta_copy(m, g)
-                beta_square(m, g)
-        transposes(0)
+                beta_mm(m, g)
+        load_copy(0)
+        load_copy(1)
+        beta_copy(0, 0)
+        beta_square(0, 1)
+        q_split(0)
+        beta_square(0, 0)
+        beta_copy(0, 1)
+        beta_copy(1, 0)
+        beta_square(1, 1)
+        beta_square(1, 0)
+        beta_copy(1, 1)
+        transposes(1)
         beta_mm(2, 0)
         beta_mm(2, 1)
-        transposes(1)
-        split_copy(0, 0, "s")
-        split_copy(0, 1, "v")
-        q_beta(0)
         q_load()
-        q_split(0)
-        for b in range(4):
+        q_beta(0)
+        for b in range(2):
             power_mm(0, b)
-        beta_copy(2, 0)
-        beta_square(2, 0)
-        beta_copy(2, 1)
-        beta_square(2, 1)
         split_copy(1, 0, "s")
         split_copy(1, 1, "s")
-        q_beta(1)
-        q_split(1)
         transposes(2)
+        for b in range(2, 4):
+            power_mm(0, b)
+        beta_copy(2, 0)
+        beta_square(2, 1)
+        beta_square(2, 0)
+        beta_copy(2, 1)
+        q_split(1)
+        q_beta(1)
         for k in range(4):
+            if k < 2:
+                split_copy(k + 2, 0, "s")
+                split_copy(k + 2, 1, "s" if k == 0 else "v")
+            if k == 0:
+                transposes(3)
             for b in range(4):
-                power_copy(k, b, "v" if b == 3 else "s")
+                power_copy(k, b, "v" if b == 3 or (k == 3 and b == 1) else "s")
             if k + 1 < 4:
                 for b in range(4):
                     power_mm(k + 1, b)
-            if k + 2 < 4:
-                split_copy(k + 2, 0, "s")
-                split_copy(k + 2, 1, "s")
-            if k + 3 < 4:
-                transposes(k + 3)
+            if k < 2:
+                q_split(k + 2)
             if k == 0:
                 q_beta(2)
             q_power(k)
-            if k + 2 < 4:
-                q_split(k + 2)
+            if k == 2:
+                stage2(0, "sg")
+                stage2(1, "sg")
+                beta_mm(3, 0)
+                beta_mm(3, 1)
+        log_sig(0)
+        log_sig(1)
+        beta_copy(3, 0)
+        beta_square(3, 1)
+        beta_square(3, 0)
+        beta_copy(3, 1)
 
         for i in range(MT):
             j = i + LEAD
-            beta = 2 < j < MT
+            beta = 3 < j < MT
+            if 3 < j + 1 < MT:
+                beta_mm(j + 1, 0)
+                beta_mm(j + 1, 1)
             stage2(i, "it")
-            stage2(i, "sg")
+            if i > 1:
+                stage2(i, "sg")
             if beta:
-                beta_mm(j, 0)
-                beta_mm(j, 1)
                 beta_copy(j, 0)
-                beta_square(j, 0)
                 beta_square(j, 1)
+                beta_square(j, 0)
             if 2 < j - 1 < MT:
                 q_beta(j - 1)
             if beta:
@@ -289,5 +313,6 @@ def tile_cell_free_log_sir_s12_kernel(tc, mix_words, mix_scales, gain_words, gai
             if i > 0:
                 finish(i - 1)
             log_int(i)
-            log_sig(i)
+            if i > 1:
+                log_sig(i)
         finish(MT - 1)

@@ -216,17 +216,18 @@ def tile_cell_free_log_sir_s12_kernel(tc, mix_words, mix_scales, gain_words, gai
                 )
 
         def log_int(m):
-            lni[m] = work.tile([P, N], F32, name="lni")
+            lni[m] = work.tile([P, N], F32, name="lni", bufs=8)
             nc.scalar.activation(out=lni[m][:], in_=itb[m][:], func=ACT.Ln)
 
-        def log_sig(m):
-            lns[m] = work.tile([P, N], F32, name="lns")
-            nc.scalar.activation(out=lns[m][:], in_=sgb[m][:], func=ACT.Ln)
+        def log_sig(m, lo=0, hi=N):
+            if lo == 0:
+                lns[m] = work.tile([P, N], F32, name="lns", bufs=8)
+            nc.scalar.activation(out=lns[m][:, lo:hi], in_=sgb[m][:, lo:hi], func=ACT.Ln)
 
-        def finish(m):
-            res = work.tile([P, N], F32, name="res")
-            nc.vector.tensor_tensor(out=res[:], in0=lns[m][:], in1=lni[m][:], op=ALU.subtract)
-            nc.sync.dma_start(out=out[m * P : (m + 1) * P, :], in_=res[:])
+        def finish(m, lo=0, hi=N):
+            res = work.tile([P, N], F32, name="res", bufs=8)
+            nc.vector.tensor_tensor(out=res[:, lo:hi], in0=lns[m][:, lo:hi], in1=lni[m][:, lo:hi], op=ALU.subtract)
+            nc.sync.dma_start(out=out[m * P : (m + 1) * P, lo:hi], in_=res[:, lo:hi])
 
         transposes(0)
         permute(0)
@@ -240,26 +241,24 @@ def tile_cell_free_log_sir_s12_kernel(tc, mix_words, mix_scales, gain_words, gai
         load_copy(1)
         beta_copy(0, 0)
         beta_square(0, 1)
-        q_split(0)
-        beta_square(0, 0)
-        beta_copy(0, 1)
         beta_copy(1, 0)
+        beta_square(0, 0)
+        q_split(0)
+        beta_copy(0, 1)
         beta_square(1, 1)
         beta_square(1, 0)
         beta_copy(1, 1)
         transposes(1)
         beta_mm(2, 0)
         beta_mm(2, 1)
+        beta_copy(2, 0)
         q_load()
         q_beta(0)
-        for b in range(2):
-            power_mm(0, b)
         split_copy(1, 0, "s")
         split_copy(1, 1, "s")
         transposes(2)
-        for b in range(2, 4):
+        for b in range(4):
             power_mm(0, b)
-        beta_copy(2, 0)
         beta_square(2, 1)
         beta_square(2, 0)
         beta_copy(2, 1)
@@ -272,7 +271,7 @@ def tile_cell_free_log_sir_s12_kernel(tc, mix_words, mix_scales, gain_words, gai
             if k == 0:
                 transposes(3)
             for b in range(4):
-                power_copy(k, b, "v" if b == 3 or (k == 3 and b == 1) else "s")
+                power_copy(k, b, "v" if b == 3 else "s")
             if k + 1 < 4:
                 for b in range(4):
                     power_mm(k + 1, b)
@@ -284,8 +283,9 @@ def tile_cell_free_log_sir_s12_kernel(tc, mix_words, mix_scales, gain_words, gai
             if k == 2:
                 stage2(0, "sg")
                 stage2(1, "sg")
-                beta_mm(3, 0)
-                beta_mm(3, 1)
+                for m in (3, 4):
+                    beta_mm(m, 0)
+                    beta_mm(m, 1)
         log_sig(0)
         log_sig(1)
         beta_copy(3, 0)
@@ -296,12 +296,15 @@ def tile_cell_free_log_sir_s12_kernel(tc, mix_words, mix_scales, gain_words, gai
         for i in range(MT):
             j = i + LEAD
             beta = 3 < j < MT
-            if 3 < j + 1 < MT:
+            if i > 1:
+                stage2(i, "it")
+                stage2(i, "sg")
+            if i == 0:
+                stage2(0, "it")
+                stage2(1, "it")
+            if 4 < j + 1 < MT:
                 beta_mm(j + 1, 0)
                 beta_mm(j + 1, 1)
-            stage2(i, "it")
-            if i > 1:
-                stage2(i, "sg")
             if beta:
                 beta_copy(j, 0)
                 beta_square(j, 1)
@@ -310,9 +313,17 @@ def tile_cell_free_log_sir_s12_kernel(tc, mix_words, mix_scales, gain_words, gai
                 q_beta(j - 1)
             if beta:
                 beta_copy(j, 1)
-            if i > 0:
-                finish(i - 1)
+            if 1 < i and i - 2 < 10:
+                finish(i - 2)
             log_int(i)
-            if i > 1:
+            if i == MT - 1:
+                log_sig(i, 0, N // 2)
+                log_sig(i, N // 2, N)
+            elif i > 1:
                 log_sig(i)
-        finish(MT - 1)
+            if i == MT - 2:
+                for m in range(10, MT - 2):
+                    finish(m)
+        finish(MT - 2)
+        finish(MT - 1, 0, N // 2)
+        finish(MT - 1, N // 2, N)

@@ -3,7 +3,7 @@ from contextlib import ExitStack
 import concourse.mybir as mybir
 from concourse.masks import make_identity
 
-M, K, A, F, N = 2048, 512, 1024, 512, 512
+USERS, ATOMS, POINTS, CLASSES, PATTERNS = 2048, 512, 1024, 512, 512
 
 F32 = mybir.dt.float32
 BF16 = mybir.dt.bfloat16
@@ -15,12 +15,24 @@ FP4X4 = mybir.dt.float4_e2m1fn_x4
 ACT = mybir.ActivationFunctionType
 ALU = mybir.AluOpType
 
-FLOPS = 2 * K * M * A + 2 * 2 * A * F * N + 2 * 2 * M * A * N
-BYTES = M * K // 2 + M * K // 32 + A * K // 2 + A * K // 32 + 2 * (2 * A * F + F * N) + 4 * M * N
+FLOPS = 2 * ATOMS * USERS * POINTS + 2 * 2 * POINTS * CLASSES * PATTERNS + 2 * 2 * USERS * POINTS * PATTERNS
+BYTES = (
+    (USERS + POINTS) * (ATOMS // 2 + ATOMS // 32)
+    + 2 * (2 * POINTS * CLASSES + CLASSES * PATTERNS)
+    + 4 * USERS * PATTERNS
+)
 
 P = 128
-MT = M // P
-LEAD = 2
+PACK = 4
+K_PASS = P * PACK
+TILES = USERS // P
+GROUPS = POINTS // K_PASS
+BLOCKS = 2 * GROUPS
+FIRST_MIX = 2 * 4 * P
+
+EARLY = 5
+AHEAD = 2
+DEFERRED = 11
 
 
 def tile_cell_free_log_sir_s12_kernel(tc, mix_words, mix_scales, gain_words, gain_scales, split, load, out):
@@ -30,300 +42,335 @@ def tile_cell_free_log_sir_s12_kernel(tc, mix_words, mix_scales, gain_words, gai
         work = ctx.enter_context(tc.tile_pool(name="work", bufs=4))
         psum = ctx.enter_context(tc.psum_pool(name="psum", bufs=2))
 
-        mixw = keep.tile([P, 2 * M], U8, name="mixw", align_bytes=64)
-        mixs = keep.tile([P, M], U8, name="mixs", align_bytes=64)
-        graw = keep.tile([P, 2 * A], U8, name="graw", align_bytes=64)
-        gsraw = keep.tile([P, A], U8, name="gsraw", align_bytes=64)
-        gw = keep.tile([P, 2 * A], U8, name="gw", align_bytes=64)
-        gs = keep.tile([P, A], U8, name="gs", align_bytes=64)
-        ident = keep.tile([P, P], F32, name="ident", align_bytes=64)
-        sp = [keep.tile([P, 4 * F], BF16, name="sp%d" % k, align_bytes=64) for k in range(4)]
-        spg = [keep.tile([P, 4 * P, 4], BF16, name="spg%d" % k, align_bytes=64) for k in range(4)]
-        spc = [keep.tile([P, 4 * P], U32, name="spc%d" % k, align_bytes=64) for k in range(4)]
-        sps = [keep.tile([P, 4 * P], U8, name="sps%d" % k, align_bytes=64) for k in range(4)]
-        lraw = keep.tile([P, 4, N], BF16, name="lraw", align_bytes=64)
-        lg = keep.tile([P, N, 4], BF16, name="lg", align_bytes=64)
-        lc = keep.tile([P, N], U32, name="lc", align_bytes=64)
-        lsc = keep.tile([P, N], U8, name="lsc", align_bytes=64)
-        pw = [keep.tile([P, N, 4], BF16, name="pw%d" % k, align_bytes=64) for k in range(4)]
-        pc = [keep.tile([P, N], U32, name="pc%d" % k, align_bytes=64) for k in range(4)]
-        ps = [keep.tile([P, N], U8, name="ps%d" % k, align_bytes=64) for k in range(4)]
-        warm = keep.tile([P, 1], F32, name="warm")
+        mix_codes = keep.tile([P, 2 * USERS], U8, name="mix_codes", align_bytes=64)
+        mix_scale = keep.tile([P, USERS], U8, name="mix_scale", align_bytes=64)
+        gain_codes_in = keep.tile([P, 2 * POINTS], U8, name="gain_codes_in", align_bytes=64)
+        gain_scale_in = keep.tile([P, POINTS], U8, name="gain_scale_in", align_bytes=64)
+        gain_codes = keep.tile([P, 2 * POINTS], U8, name="gain_codes", align_bytes=64)
+        gain_scale = keep.tile([P, POINTS], U8, name="gain_scale", align_bytes=64)
 
-        mix_w = mix_words.rearrange("o p b -> (o p) b")
-        mix_s = mix_scales.rearrange("o q n -> (o q) n")
-        gain_w = gain_words.rearrange("o p b -> (o p) b")
-        gain_s = gain_scales.rearrange("o q n -> (o q) n")
+        split_in = [keep.tile([P, PACK * CLASSES], BF16, name="split_in%d" % k, align_bytes=64) for k in range(BLOCKS)]
+        split_bf = [keep.tile([P, K_PASS, PACK], BF16, name="split_bf%d" % k, align_bytes=64) for k in range(BLOCKS)]
+        split_codes = [keep.tile([P, K_PASS], U32, name="split_codes%d" % k, align_bytes=64) for k in range(BLOCKS)]
+        split_scale = [keep.tile([P, K_PASS], U8, name="split_scale%d" % k, align_bytes=64) for k in range(BLOCKS)]
+        load_in = keep.tile([P, PACK, PATTERNS], BF16, name="load_in", align_bytes=64)
+        load_bf = keep.tile([P, PATTERNS, PACK], BF16, name="load_bf", align_bytes=64)
+        load_codes = keep.tile([P, PATTERNS], U32, name="load_codes", align_bytes=64)
+        load_scale = keep.tile([P, PATTERNS], U8, name="load_scale", align_bytes=64)
+        power_bf = [keep.tile([P, PATTERNS, PACK], BF16, name="power_bf%d" % k, align_bytes=64) for k in range(BLOCKS)]
+        power_codes = [keep.tile([P, PATTERNS], U32, name="power_codes%d" % k, align_bytes=64) for k in range(BLOCKS)]
+        power_scale = [keep.tile([P, PATTERNS], U8, name="power_scale%d" % k, align_bytes=64) for k in range(BLOCKS)]
+
+        identity = keep.tile([P, P], F32, name="identity", align_bytes=64)
+        one = keep.tile([P, 1], F32, name="one")
+
+        mix_words_2d = mix_words.rearrange("o p b -> (o p) b")
+        mix_scales_2d = mix_scales.rearrange("o q n -> (o q) n")
+        gain_words_2d = gain_words.rearrange("o p b -> (o p) b")
+        gain_scales_2d = gain_scales.rearrange("o q n -> (o q) n")
 
         ctx.enter_context(tc.manual_schedule())
 
-        nc.vector.memset(gsraw[:].bitcast(I32), 0)
-        nc.vector.memset(mixs[:].bitcast(I32), 0)
-        nc.vector.memset(warm[:], 1.0)
-        nc.scalar.activation(out=warm[:], in_=warm[:], func=ACT.Ln)
-        make_identity(nc, ident[:])
+
+        def load_mix(lo, hi):
+            nc.sync.dma_start(out=mix_codes[:, lo:hi].bitcast(I32), in_=mix_words_2d[:, lo:hi].bitcast(I32))
+
+        def load_scales(scale, source):
+            for r in range(4):
+                nc.sync.dma_start(out=scale[r:P:32, :].bitcast(I32), in_=source[r:16:4, :].bitcast(I32))
 
         def load_split(k):
-            nc.sync.dma_start(out=sp[k][:], in_=split[512 * k : 512 * (k + 1), :].rearrange("(p s) f -> p (s f)", s=4))
+            rows = split[k * K_PASS : (k + 1) * K_PASS, :]
+            nc.sync.dma_start(out=split_in[k][:], in_=rows.rearrange("(p s) f -> p (s f)", s=PACK))
 
-        def load_mix(a, b):
-            nc.sync.dma_start(out=mixw[:, a:b].bitcast(I32), in_=mix_w[:, a:b].bitcast(I32))
+        nc.vector.memset(gain_scale_in[:].bitcast(I32), 0)
+        nc.vector.memset(mix_scale[:].bitcast(I32), 0)
+        nc.vector.memset(one[:], 1.0)
+        nc.scalar.activation(out=one[:], in_=one[:], func=ACT.Ln)
+        make_identity(nc, identity[:])
 
+        nc.sync.dma_start(out=gain_codes_in[:].bitcast(I32), in_=gain_words_2d.bitcast(I32))
+        load_mix(0, FIRST_MIX)
+        load_scales(gain_scale_in, gain_scales_2d)
+        load_scales(mix_scale, mix_scales_2d)
+        nc.sync.dma_start(out=load_in[:], in_=load.rearrange("(p j) n -> p j n", j=PACK))
         load_split(0)
-        nc.sync.dma_start(out=graw[:].bitcast(I32), in_=gain_w.bitcast(I32))
-        for r in range(4):
-            nc.sync.dma_start(out=gsraw[r:P:32, :].bitcast(I32), in_=gain_s[r:16:4, :].bitcast(I32))
-        load_mix(0, 1024)
-        for r in range(4):
-            nc.sync.dma_start(out=mixs[r:P:32, :].bitcast(I32), in_=mix_s[r:16:4, :].bitcast(I32))
-        nc.sync.dma_start(out=lraw[:], in_=load.rearrange("(p j) n -> p j n", j=4))
         load_split(1)
-        load_mix(1024, 4096)
+        load_mix(FIRST_MIX, 2 * USERS)
         load_split(2)
         load_split(3)
 
-        def permute(g):
+
+        def quantize(codes, scale, values):
+            nc.vector.quantize_mx(out=codes.bitcast(FP8X4), scales=scale, in_=values)
+
+        def reorder_gain_codes(g):
+            lo, hi = 2 * K_PASS * g, 2 * K_PASS * (g + 1)
             nc.vector.tensor_copy(
-                out=gs[:, 512 * g : 512 * (g + 1)].rearrange("p (t x y) -> p t x y", t=4, y=2),
-                in_=gsraw[:, 512 * g : 512 * (g + 1)].rearrange("p (x t y) -> p t x y", t=4, y=2),
-            )
-            nc.vector.tensor_copy(
-                out=gw[:, 1024 * g : 1024 * (g + 1)].bitcast(I32).rearrange("p (t x) -> p t x", t=4),
-                in_=graw[:, 1024 * g : 1024 * (g + 1)].bitcast(I32).rearrange("p (x t) -> p t x", t=4),
+                out=gain_codes[:, lo:hi].bitcast(I32).rearrange("p (t x) -> p t x", t=PACK),
+                in_=gain_codes_in[:, lo:hi].bitcast(I32).rearrange("p (x t) -> p t x", t=PACK),
             )
 
-        wbank = {}
-        bt, bq = {}, {}
+        def reorder_gain_scales(g):
+            lo, hi = K_PASS * g, K_PASS * (g + 1)
+            nc.vector.tensor_copy(
+                out=gain_scale[:, lo:hi].rearrange("p (t x y) -> p t x y", t=PACK, y=2),
+                in_=gain_scale_in[:, lo:hi].rearrange("p (x t y) -> p t x y", t=PACK, y=2),
+            )
 
-        def beta_mm(m, g):
+        beta_bank, beta_bf, beta_q = {}, {}, {}
+
+        def multiply_beta(m, g):
             if g == 0:
-                bt[m] = work.tile([P, 2, 2, P, 4], BF16, name="bt", align_bytes=64)
-            w = psum.tile([P, 4, P], F32, name="w", bufs=4)
-            wbank[(m, g)] = w
-            for t in range(4):
-                c = (4 * g + t) * P
+                beta_bf[m] = work.tile([P, 2, GROUPS, P, PACK], BF16, name="beta_bf", align_bytes=64)
+            bank = psum.tile([P, PACK, P], F32, name="first", bufs=4)
+            beta_bank[(m, g)] = bank
+            for t in range(PACK):
+                c = (PACK * g + t) * P
                 nc.tensor.matmul_mx(
-                    out=w[:, t, :],
-                    lhsT=gw[:, 2 * c : 2 * (c + P)].bitcast(FP4X4),
-                    lhsT_scale=gs[:, c : c + P],
-                    rhs=mixw[:, 2 * m * P : 2 * (m + 1) * P].bitcast(FP4X4),
-                    rhs_scale=mixs[:, m * P : (m + 1) * P],
+                    out=bank[:, t, :],
+                    lhsT=gain_codes[:, 2 * c : 2 * (c + P)].bitcast(FP4X4),
+                    lhsT_scale=gain_scale[:, c : c + P],
+                    rhs=mix_codes[:, 2 * m * P : 2 * (m + 1) * P].bitcast(FP4X4),
+                    rhs_scale=mix_scale[:, m * P : (m + 1) * P],
                     start=(t == 0),
-                    stop=(t == 3),
+                    stop=(t == PACK - 1),
                 )
 
-        def beta_copy(m, g):
-            nc.vector.tensor_copy(out=bt[m][:, 1, g], in_=wbank[(m, g)][:].rearrange("p t u -> p u t"))
 
-        def beta_square(m, g):
-            nc.scalar.activation(out=bt[m][:, 0, g], in_=wbank[(m, g)][:].rearrange("p t u -> p u t"), func=ACT.Square)
+        def square_beta(m, g):
+            bank = beta_bank[(m, g)]
+            nc.scalar.activation(out=beta_bf[m][:, 0, g], in_=bank[:].rearrange("p t u -> p u t"), func=ACT.Square)
 
-        def quant(dst_c, dst_s, src):
-            nc.vector.quantize_mx(out=dst_c.bitcast(FP8X4), scales=dst_s, in_=src)
+        def copy_beta(m, g):
+            bank = beta_bank[(m, g)]
+            nc.vector.tensor_copy(out=beta_bf[m][:, 1, g], in_=bank[:].rearrange("p t u -> p u t"))
 
-        def q_beta(m):
-            c = work.tile([P, 4 * P], U32, name="bc", align_bytes=64)
-            s = work.tile([P, 4 * P], U8, name="bs", align_bytes=64)
-            bq[m] = (c, s)
-            quant(c[:], s[:], bt[m][:].rearrange("p a g u t -> p (a g u t)"))
+        def quantize_beta(m):
+            codes = work.tile([P, 2 * GROUPS * P], U32, name="beta_codes", align_bytes=64)
+            scale = work.tile([P, 2 * GROUPS * P], U8, name="beta_scale", align_bytes=64)
+            beta_q[m] = (codes, scale)
+            quantize(codes[:], scale[:], beta_bf[m][:].rearrange("p a g u t -> p (a g u t)"))
 
-        tbank = {}
+        split_bank = {}
 
-        def transposes(k):
-            words = sp[k][:].bitcast(F32)
+        def transpose_split(k):
+            pairs = split_in[k][:].bitcast(F32)
+            row = CLASSES // 2
             for h in range(2):
                 if h == 0:
-                    b = psum.tile([P, 4, P], F32, name="sg", bufs=2)
+                    bank = psum.tile([P, 4, P], F32, name="signal")
                 else:
-                    b = psum.tile([P, 4, P], F32, name="it", bufs=2)
-                tbank[(k, h)] = b
+                    bank = psum.tile([P, 4, P], F32, name="interference")
+                split_bank[(k, h)] = bank
                 for y in range(2):
                     for u in range(2):
-                        o = (2 * h + y) * 256 + u
-                        nc.tensor.transpose(b[:, 2 * y + u, :], words[:, o : o + 255 : 2], ident[:])
+                        lo = (2 * h + y) * row + u
+                        nc.tensor.transpose(bank[:, 2 * y + u, :], pairs[:, lo : lo + row - 1 : 2], identity[:])
 
-        def split_copy(k, h, eng):
-            dst = spg[k][:].rearrange("p c j -> p (c j)").bitcast(F32).rearrange("p (a h x v) -> p h a x v", a=2, h=2, v=4)[:, h]
-            src = tbank[(k, h)][:].rearrange("p v (x a) -> p a x v", a=2)
-            if eng == "s":
-                nc.scalar.copy(out=dst, in_=src)
-            else:
+        def copy_split(k, h):
+            pairs = split_bf[k][:].rearrange("p c j -> p (c j)").bitcast(F32)
+            dst = pairs.rearrange("p (a h x v) -> p h a x v", a=2, h=2, v=4)[:, h]
+            src = split_bank[(k, h)][:].rearrange("p v (x a) -> p a x v", a=2)
+            if h == 1 and k % 2 == 1:
                 nc.vector.tensor_copy(out=dst, in_=src)
+            else:
+                nc.scalar.copy(out=dst, in_=src)
 
-        def q_split(k):
-            quant(spc[k][:], sps[k][:], spg[k][:].rearrange("p c j -> p (c j)"))
+        def quantize_split(k):
+            quantize(split_codes[k][:], split_scale[k][:], split_bf[k][:].rearrange("p c j -> p (c j)"))
 
-        def load_copy(i):
-            c = slice(256 * i, 256 * (i + 1))
+        def interleave_load(half):
+            n = slice(half * PATTERNS // 2, (half + 1) * PATTERNS // 2)
             nc.gpsimd.tensor_scalar(
-                out=lg[:, c, :],
-                in0=lraw[:, :, c].rearrange("p t n -> p n t"),
+                out=load_bf[:, n, :],
+                in0=load_in[:, :, n].rearrange("p j n -> p n j"),
                 scalar1=1.0,
                 scalar2=0.0,
                 op0=ALU.mult,
                 op1=ALU.add,
             )
 
-        def q_load():
-            quant(lc[:], lsc[:], lg[:].rearrange("p n j -> p (n j)"))
+        def quantize_load():
+            quantize(load_codes[:], load_scale[:], load_bf[:].rearrange("p n j -> p (n j)"))
 
-        pbank = {}
+        power_bank = {}
 
-        def power_mm(k, b):
-            w = psum.tile([P, 4, P], F32, name="w", bufs=4)
-            pbank[(k, b)] = w
-            for t in range(4):
-                nc.tensor.matmul_mx(
-                    out=w[:, t, :],
-                    lhsT=spc[k][:, t * P : (t + 1) * P].bitcast(FP8X4),
-                    lhsT_scale=sps[k][:, t * P : (t + 1) * P],
-                    rhs=lc[:, b * P : (b + 1) * P].bitcast(FP8X4),
-                    rhs_scale=lsc[:, b * P : (b + 1) * P],
-                    start=True,
-                    stop=True,
-                )
+        def multiply_power(k):
+            for b in range(4):
+                n = slice(b * P, (b + 1) * P)
+                bank = psum.tile([P, PACK, P], F32, name="first", bufs=4)
+                power_bank[(k, b)] = bank
+                for t in range(PACK):
+                    c = slice(t * P, (t + 1) * P)
+                    nc.tensor.matmul_mx(
+                        out=bank[:, t, :],
+                        lhsT=split_codes[k][:, c].bitcast(FP8X4),
+                        lhsT_scale=split_scale[k][:, c],
+                        rhs=load_codes[:, n].bitcast(FP8X4),
+                        rhs_scale=load_scale[:, n],
+                        start=True,
+                        stop=True,
+                    )
 
-        def power_copy(k, b, eng):
-            dst = pw[k][:, b * P : (b + 1) * P, :]
-            src = pbank[(k, b)][:].rearrange("p t n -> p n t")
-            if eng == "s":
-                nc.scalar.copy(out=dst, in_=src)
-            else:
-                nc.vector.tensor_copy(out=dst, in_=src)
+        def copy_power(k):
+            for b in range(4):
+                dst = power_bf[k][:, b * P : (b + 1) * P, :]
+                src = power_bank[(k, b)][:].rearrange("p t n -> p n t")
+                if b == 3:
+                    nc.vector.tensor_copy(out=dst, in_=src)
+                else:
+                    nc.scalar.copy(out=dst, in_=src)
 
-        def q_power(k):
-            quant(pc[k][:], ps[k][:], pw[k][:].rearrange("p n t -> p (n t)"))
+        def quantize_power(k):
+            quantize(power_codes[k][:], power_scale[k][:], power_bf[k][:].rearrange("p n t -> p (n t)"))
 
-        sgb, itb, lns, lni = {}, {}, {}, {}
+        signal, interference, log_signal, log_interference = {}, {}, {}, {}
 
-        def stage2(m, which):
-            base = 0 if which == "sg" else 2
-            if which == "sg":
-                acc = psum.tile([P, N], F32, name="sg", bufs=2)
-                sgb[m] = acc
-            else:
-                acc = psum.tile([P, N], F32, name="it", bufs=2)
-                itb[m] = acc
-            for g in range(2):
+        def contract_points(acc, m, a):
+            codes, scale = beta_q[m]
+            for g in range(GROUPS):
+                c = slice((GROUPS * a + g) * P, (GROUPS * a + g + 1) * P)
+                k = GROUPS * a + g
                 nc.tensor.matmul_mx(
                     out=acc[:],
-                    lhsT=bq[m][0][:, (base + g) * P : (base + g + 1) * P].bitcast(FP8X4),
-                    lhsT_scale=bq[m][1][:, (base + g) * P : (base + g + 1) * P],
-                    rhs=pc[base + g][:].bitcast(FP8X4),
-                    rhs_scale=ps[base + g][:],
+                    lhsT=codes[:, c].bitcast(FP8X4),
+                    lhsT_scale=scale[:, c],
+                    rhs=power_codes[k][:].bitcast(FP8X4),
+                    rhs_scale=power_scale[k][:],
                     start=(g == 0),
-                    stop=(g == 1),
+                    stop=(g == GROUPS - 1),
                 )
 
-        def log_int(m):
-            lni[m] = work.tile([P, N], F32, name="lni", bufs=8)
-            nc.scalar.activation(out=lni[m][:], in_=itb[m][:], func=ACT.Ln)
+        def multiply_signal(m):
+            signal[m] = psum.tile([P, PATTERNS], F32, name="signal")
+            contract_points(signal[m], m, 0)
 
-        def log_sig(m, lo=0, hi=N):
-            if lo == 0:
-                lns[m] = work.tile([P, N], F32, name="lns", bufs=8)
-            nc.scalar.activation(out=lns[m][:, lo:hi], in_=sgb[m][:, lo:hi], func=ACT.Ln)
+        def multiply_interference(m):
+            interference[m] = psum.tile([P, PATTERNS], F32, name="interference")
+            contract_points(interference[m], m, 1)
 
-        def finish(m, lo=0, hi=N):
-            res = work.tile([P, N], F32, name="res", bufs=8)
-            nc.vector.tensor_tensor(out=res[:, lo:hi], in0=lns[m][:, lo:hi], in1=lni[m][:, lo:hi], op=ALU.subtract)
-            nc.sync.dma_start(out=out[m * P : (m + 1) * P, lo:hi], in_=res[:, lo:hi])
+        def take_log_interference(m):
+            log_interference[m] = work.tile([P, PATTERNS], F32, name="log_interference", bufs=8)
+            nc.scalar.activation(out=log_interference[m][:], in_=interference[m][:], func=ACT.Ln)
 
-        transposes(0)
-        permute(0)
-        permute(1)
-        split_copy(0, 0, "s")
-        split_copy(0, 1, "s")
+        def take_log_signal(m, pieces=1):
+            log_signal[m] = work.tile([P, PATTERNS], F32, name="log_signal", bufs=8)
+            for i in range(pieces):
+                n = slice(i * PATTERNS // pieces, (i + 1) * PATTERNS // pieces)
+                nc.scalar.activation(out=log_signal[m][:, n], in_=signal[m][:, n], func=ACT.Ln)
+
+        def finish(m, pieces=1):
+            for i in range(pieces):
+                n = slice(i * PATTERNS // pieces, (i + 1) * PATTERNS // pieces)
+                result = work.tile([P, PATTERNS], F32, name="result", bufs=8)
+                nc.vector.tensor_tensor(
+                    out=result[:, n], in0=log_signal[m][:, n], in1=log_interference[m][:, n], op=ALU.subtract
+                )
+                nc.sync.dma_start(out=out[m * P : (m + 1) * P, n], in_=result[:, n])
+
+
+        for g in range(GROUPS):
+            reorder_gain_codes(g)
+        for g in range(GROUPS):
+            reorder_gain_scales(g)
         for m in (0, 1):
-            for g in range(2):
-                beta_mm(m, g)
-        load_copy(0)
-        load_copy(1)
-        beta_copy(0, 0)
-        beta_square(0, 1)
-        beta_copy(1, 0)
-        beta_square(0, 0)
-        q_split(0)
-        beta_copy(0, 1)
-        beta_square(1, 1)
-        beta_square(1, 0)
-        beta_copy(1, 1)
-        transposes(1)
-        beta_mm(2, 0)
-        beta_mm(2, 1)
-        beta_copy(2, 0)
-        q_load()
-        q_beta(0)
-        split_copy(1, 0, "s")
-        split_copy(1, 1, "s")
-        transposes(2)
-        for b in range(4):
-            power_mm(0, b)
-        beta_square(2, 1)
-        beta_square(2, 0)
-        beta_copy(2, 1)
-        q_split(1)
-        q_beta(1)
-        for k in range(4):
-            if k < 2:
-                split_copy(k + 2, 0, "s")
-                split_copy(k + 2, 1, "s" if k == 0 else "v")
-            if k == 0:
-                transposes(3)
-            for b in range(4):
-                power_copy(k, b, "v" if b == 3 else "s")
-            if k + 1 < 4:
-                for b in range(4):
-                    power_mm(k + 1, b)
-            if k < 2:
-                q_split(k + 2)
-            if k == 0:
-                q_beta(2)
-            q_power(k)
-            if k == 2:
-                stage2(0, "sg")
-                stage2(1, "sg")
-                for m in (3, 4):
-                    beta_mm(m, 0)
-                    beta_mm(m, 1)
-        log_sig(0)
-        log_sig(1)
-        beta_copy(3, 0)
-        beta_square(3, 1)
-        beta_square(3, 0)
-        beta_copy(3, 1)
+            for g in range(GROUPS):
+                multiply_beta(m, g)
+        copy_beta(0, 0)
+        square_beta(0, 1)
+        square_beta(0, 0)
+        copy_beta(1, 0)
+        copy_beta(0, 1)
+        square_beta(1, 1)
+        square_beta(1, 0)
+        copy_beta(1, 1)
+        interleave_load(0)
+        interleave_load(1)
+        multiply_beta(2, 0)
+        multiply_beta(2, 1)
+        transpose_split(0)
+        transpose_split(1)
+        square_beta(2, 1)
+        copy_beta(2, 0)
+        square_beta(2, 0)
+        copy_beta(2, 1)
+        copy_split(0, 0)
+        copy_split(0, 1)
+        quantize_beta(0)
+        quantize_load()
+        quantize_split(0)
+        transpose_split(2)
+        multiply_power(0)
+        copy_split(1, 0)
+        copy_split(1, 1)
+        quantize_beta(1)
+        quantize_split(1)
 
-        for i in range(MT):
-            j = i + LEAD
-            beta = 3 < j < MT
-            if i > 1:
-                stage2(i, "it")
-                stage2(i, "sg")
+        copy_split(2, 0)
+        copy_split(2, 1)
+        transpose_split(3)
+        quantize_beta(2)
+        copy_power(0)
+        multiply_power(1)
+        quantize_split(2)
+        quantize_power(0)
+
+        copy_split(3, 0)
+        copy_split(3, 1)
+        copy_power(1)
+        multiply_power(2)
+        quantize_split(3)
+        quantize_power(1)
+
+        copy_power(2)
+        multiply_power(3)
+        quantize_power(2)
+
+        multiply_signal(0)
+        multiply_signal(1)
+        for m in range(3, EARLY):
+            for g in range(GROUPS):
+                multiply_beta(m, g)
+        copy_power(3)
+        quantize_power(3)
+        take_log_signal(0)
+        take_log_signal(1)
+        copy_beta(3, 0)
+        square_beta(3, 1)
+        square_beta(3, 0)
+        copy_beta(4, 0)
+        copy_beta(3, 1)
+
+
+        for i in range(TILES):
+            j = i + AHEAD
             if i == 0:
-                stage2(0, "it")
-                stage2(1, "it")
-            if 4 < j + 1 < MT:
-                beta_mm(j + 1, 0)
-                beta_mm(j + 1, 1)
-            if beta:
-                beta_copy(j, 0)
-                beta_square(j, 1)
-                beta_square(j, 0)
-            if 2 < j - 1 < MT:
-                q_beta(j - 1)
-            if beta:
-                beta_copy(j, 1)
-            if 1 < i and i - 2 < 10:
-                finish(i - 2)
-            log_int(i)
-            if i == MT - 1:
-                log_sig(i, 0, N // 2)
-                log_sig(i, N // 2, N)
+                multiply_interference(0)
+                multiply_interference(1)
             elif i > 1:
-                log_sig(i)
-            if i == MT - 2:
-                for m in range(10, MT - 2):
+                multiply_interference(i)
+                multiply_signal(i)
+            if EARLY <= j + 1 < TILES:
+                for g in range(GROUPS):
+                    multiply_beta(j + 1, g)
+            beta = EARLY - 1 <= j < TILES
+            if beta:
+                if j >= EARLY:
+                    copy_beta(j, 0)
+                square_beta(j, 1)
+                square_beta(j, 0)
+            if EARLY - 2 <= j - 1 < TILES:
+                quantize_beta(j - 1)
+            if 0 <= i - 2 < DEFERRED:
+                finish(i - 2)
+            if beta:
+                copy_beta(j, 1)
+            take_log_interference(i)
+            if i > 1:
+                take_log_signal(i, pieces=2 if i == TILES - 1 else 1)
+            if i == TILES - 2:
+                for m in range(DEFERRED, TILES - 2):
                     finish(m)
-        finish(MT - 2)
-        finish(MT - 1, 0, N // 2)
-        finish(MT - 1, N // 2, N)
+        finish(TILES - 2)
+        finish(TILES - 1, pieces=2)

from contextlib import ExitStack

import concourse.mybir as mybir
from concourse.masks import make_identity

USERS, ATOMS, POINTS, CLASSES, PATTERNS = 2048, 512, 1024, 512, 512

F32 = mybir.dt.float32
BF16 = mybir.dt.bfloat16
I32 = mybir.dt.int32
U32 = mybir.dt.uint32
U8 = mybir.dt.uint8
FP8X4 = mybir.dt.float8_e4m3fn_x4
FP4X4 = mybir.dt.float4_e2m1fn_x4
ACT = mybir.ActivationFunctionType
ALU = mybir.AluOpType

FLOPS = 2 * ATOMS * USERS * POINTS + 2 * 2 * POINTS * CLASSES * PATTERNS + 2 * 2 * USERS * POINTS * PATTERNS
BYTES = (
    (USERS + POINTS) * (ATOMS // 2 + ATOMS // 32)
    + 2 * (2 * POINTS * CLASSES + CLASSES * PATTERNS)
    + 4 * USERS * PATTERNS
)

P = 128
PACK = 4
K_PASS = P * PACK
TILES = USERS // P
GROUPS = POINTS // K_PASS
BLOCKS = 2 * GROUPS
FIRST_MIX = 2 * 4 * P

EARLY = 5
AHEAD = 2
DEFERRED = 11


def tile_cell_free_log_sir_s12_kernel(tc, mix_words, mix_scales, gain_words, gain_scales, split, load, out):
    nc = tc.nc
    with ExitStack() as ctx:
        keep = ctx.enter_context(tc.tile_pool(name="keep", bufs=1))
        work = ctx.enter_context(tc.tile_pool(name="work", bufs=4))
        psum = ctx.enter_context(tc.psum_pool(name="psum", bufs=2))

        mix_codes = keep.tile([P, 2 * USERS], U8, name="mix_codes", align_bytes=64)
        mix_scale = keep.tile([P, USERS], U8, name="mix_scale", align_bytes=64)
        gain_codes_in = keep.tile([P, 2 * POINTS], U8, name="gain_codes_in", align_bytes=64)
        gain_scale_in = keep.tile([P, POINTS], U8, name="gain_scale_in", align_bytes=64)
        gain_codes = keep.tile([P, 2 * POINTS], U8, name="gain_codes", align_bytes=64)
        gain_scale = keep.tile([P, POINTS], U8, name="gain_scale", align_bytes=64)

        split_in = [keep.tile([P, PACK * CLASSES], BF16, name="split_in%d" % k, align_bytes=64) for k in range(BLOCKS)]
        split_bf = [keep.tile([P, K_PASS, PACK], BF16, name="split_bf%d" % k, align_bytes=64) for k in range(BLOCKS)]
        split_codes = [keep.tile([P, K_PASS], U32, name="split_codes%d" % k, align_bytes=64) for k in range(BLOCKS)]
        split_scale = [keep.tile([P, K_PASS], U8, name="split_scale%d" % k, align_bytes=64) for k in range(BLOCKS)]
        load_in = keep.tile([P, PACK, PATTERNS], BF16, name="load_in", align_bytes=64)
        load_bf = keep.tile([P, PATTERNS, PACK], BF16, name="load_bf", align_bytes=64)
        load_codes = keep.tile([P, PATTERNS], U32, name="load_codes", align_bytes=64)
        load_scale = keep.tile([P, PATTERNS], U8, name="load_scale", align_bytes=64)
        power_bf = [keep.tile([P, PATTERNS, PACK], BF16, name="power_bf%d" % k, align_bytes=64) for k in range(BLOCKS)]
        power_codes = [keep.tile([P, PATTERNS], U32, name="power_codes%d" % k, align_bytes=64) for k in range(BLOCKS)]
        power_scale = [keep.tile([P, PATTERNS], U8, name="power_scale%d" % k, align_bytes=64) for k in range(BLOCKS)]

        identity = keep.tile([P, P], F32, name="identity", align_bytes=64)
        one = keep.tile([P, 1], F32, name="one")

        mix_words_2d = mix_words.rearrange("o p b -> (o p) b")
        mix_scales_2d = mix_scales.rearrange("o q n -> (o q) n")
        gain_words_2d = gain_words.rearrange("o p b -> (o p) b")
        gain_scales_2d = gain_scales.rearrange("o q n -> (o q) n")

        ctx.enter_context(tc.manual_schedule())


        def load_mix(lo, hi):
            nc.sync.dma_start(out=mix_codes[:, lo:hi].bitcast(I32), in_=mix_words_2d[:, lo:hi].bitcast(I32))

        def load_scales(scale, source):
            for r in range(4):
                nc.sync.dma_start(out=scale[r:P:32, :].bitcast(I32), in_=source[r:16:4, :].bitcast(I32))

        def load_split(k):
            rows = split[k * K_PASS : (k + 1) * K_PASS, :]
            nc.sync.dma_start(out=split_in[k][:], in_=rows.rearrange("(p s) f -> p (s f)", s=PACK))

        nc.vector.memset(gain_scale_in[:].bitcast(I32), 0)
        nc.vector.memset(mix_scale[:].bitcast(I32), 0)
        nc.vector.memset(one[:], 1.0)
        nc.scalar.activation(out=one[:], in_=one[:], func=ACT.Ln)
        make_identity(nc, identity[:])

        nc.sync.dma_start(out=gain_codes_in[:].bitcast(I32), in_=gain_words_2d.bitcast(I32))
        load_mix(0, FIRST_MIX)
        load_scales(gain_scale_in, gain_scales_2d)
        load_scales(mix_scale, mix_scales_2d)
        nc.sync.dma_start(out=load_in[:], in_=load.rearrange("(p j) n -> p j n", j=PACK))
        load_split(0)
        load_split(1)
        load_mix(FIRST_MIX, 2 * USERS)
        load_split(2)
        load_split(3)


        def quantize(codes, scale, values):
            nc.vector.quantize_mx(out=codes.bitcast(FP8X4), scales=scale, in_=values)

        def reorder_gain_codes(g):
            lo, hi = 2 * K_PASS * g, 2 * K_PASS * (g + 1)
            nc.vector.tensor_copy(
                out=gain_codes[:, lo:hi].bitcast(I32).rearrange("p (t x) -> p t x", t=PACK),
                in_=gain_codes_in[:, lo:hi].bitcast(I32).rearrange("p (x t) -> p t x", t=PACK),
            )

        def reorder_gain_scales(g):
            lo, hi = K_PASS * g, K_PASS * (g + 1)
            nc.vector.tensor_copy(
                out=gain_scale[:, lo:hi].rearrange("p (t x y) -> p t x y", t=PACK, y=2),
                in_=gain_scale_in[:, lo:hi].rearrange("p (x t y) -> p t x y", t=PACK, y=2),
            )

        beta_bank, beta_bf, beta_q = {}, {}, {}

        def multiply_beta(m, g):
            if g == 0:
                beta_bf[m] = work.tile([P, 2, GROUPS, P, PACK], BF16, name="beta_bf", align_bytes=64)
            bank = psum.tile([P, PACK, P], F32, name="first", bufs=4)
            beta_bank[(m, g)] = bank
            for t in range(PACK):
                c = (PACK * g + t) * P
                nc.tensor.matmul_mx(
                    out=bank[:, t, :],
                    lhsT=gain_codes[:, 2 * c : 2 * (c + P)].bitcast(FP4X4),
                    lhsT_scale=gain_scale[:, c : c + P],
                    rhs=mix_codes[:, 2 * m * P : 2 * (m + 1) * P].bitcast(FP4X4),
                    rhs_scale=mix_scale[:, m * P : (m + 1) * P],
                    start=(t == 0),
                    stop=(t == PACK - 1),
                )


        def square_beta(m, g):
            bank = beta_bank[(m, g)]
            nc.scalar.activation(out=beta_bf[m][:, 0, g], in_=bank[:].rearrange("p t u -> p u t"), func=ACT.Square)

        def copy_beta(m, g):
            bank = beta_bank[(m, g)]
            nc.vector.tensor_copy(out=beta_bf[m][:, 1, g], in_=bank[:].rearrange("p t u -> p u t"))

        def quantize_beta(m):
            codes = work.tile([P, 2 * GROUPS * P], U32, name="beta_codes", align_bytes=64)
            scale = work.tile([P, 2 * GROUPS * P], U8, name="beta_scale", align_bytes=64)
            beta_q[m] = (codes, scale)
            quantize(codes[:], scale[:], beta_bf[m][:].rearrange("p a g u t -> p (a g u t)"))

        split_bank = {}

        def transpose_split(k):
            pairs = split_in[k][:].bitcast(F32)
            row = CLASSES // 2
            for h in range(2):
                if h == 0:
                    bank = psum.tile([P, 4, P], F32, name="signal")
                else:
                    bank = psum.tile([P, 4, P], F32, name="interference")
                split_bank[(k, h)] = bank
                for y in range(2):
                    for u in range(2):
                        lo = (2 * h + y) * row + u
                        nc.tensor.transpose(bank[:, 2 * y + u, :], pairs[:, lo : lo + row - 1 : 2], identity[:])

        def copy_split(k, h):
            pairs = split_bf[k][:].rearrange("p c j -> p (c j)").bitcast(F32)
            dst = pairs.rearrange("p (a h x v) -> p h a x v", a=2, h=2, v=4)[:, h]
            src = split_bank[(k, h)][:].rearrange("p v (x a) -> p a x v", a=2)
            if h == 1 and k % 2 == 1:
                nc.vector.tensor_copy(out=dst, in_=src)
            else:
                nc.scalar.copy(out=dst, in_=src)

        def quantize_split(k):
            quantize(split_codes[k][:], split_scale[k][:], split_bf[k][:].rearrange("p c j -> p (c j)"))

        def interleave_load(half):
            n = slice(half * PATTERNS // 2, (half + 1) * PATTERNS // 2)
            nc.gpsimd.tensor_scalar(
                out=load_bf[:, n, :],
                in0=load_in[:, :, n].rearrange("p j n -> p n j"),
                scalar1=1.0,
                scalar2=0.0,
                op0=ALU.mult,
                op1=ALU.add,
            )

        def quantize_load():
            quantize(load_codes[:], load_scale[:], load_bf[:].rearrange("p n j -> p (n j)"))

        power_bank = {}

        def multiply_power(k):
            for b in range(4):
                n = slice(b * P, (b + 1) * P)
                bank = psum.tile([P, PACK, P], F32, name="first", bufs=4)
                power_bank[(k, b)] = bank
                for t in range(PACK):
                    c = slice(t * P, (t + 1) * P)
                    nc.tensor.matmul_mx(
                        out=bank[:, t, :],
                        lhsT=split_codes[k][:, c].bitcast(FP8X4),
                        lhsT_scale=split_scale[k][:, c],
                        rhs=load_codes[:, n].bitcast(FP8X4),
                        rhs_scale=load_scale[:, n],
                        start=True,
                        stop=True,
                    )

        def copy_power(k):
            for b in range(4):
                dst = power_bf[k][:, b * P : (b + 1) * P, :]
                src = power_bank[(k, b)][:].rearrange("p t n -> p n t")
                if b == 3:
                    nc.vector.tensor_copy(out=dst, in_=src)
                else:
                    nc.scalar.copy(out=dst, in_=src)

        def quantize_power(k):
            quantize(power_codes[k][:], power_scale[k][:], power_bf[k][:].rearrange("p n t -> p (n t)"))

        signal, interference, log_signal, log_interference = {}, {}, {}, {}

        def contract_points(acc, m, a):
            codes, scale = beta_q[m]
            for g in range(GROUPS):
                c = slice((GROUPS * a + g) * P, (GROUPS * a + g + 1) * P)
                k = GROUPS * a + g
                nc.tensor.matmul_mx(
                    out=acc[:],
                    lhsT=codes[:, c].bitcast(FP8X4),
                    lhsT_scale=scale[:, c],
                    rhs=power_codes[k][:].bitcast(FP8X4),
                    rhs_scale=power_scale[k][:],
                    start=(g == 0),
                    stop=(g == GROUPS - 1),
                )

        def multiply_signal(m):
            signal[m] = psum.tile([P, PATTERNS], F32, name="signal")
            contract_points(signal[m], m, 0)

        def multiply_interference(m):
            interference[m] = psum.tile([P, PATTERNS], F32, name="interference")
            contract_points(interference[m], m, 1)

        def take_log_interference(m):
            log_interference[m] = work.tile([P, PATTERNS], F32, name="log_interference", bufs=8)
            nc.scalar.activation(out=log_interference[m][:], in_=interference[m][:], func=ACT.Ln)

        def take_log_signal(m, pieces=1):
            log_signal[m] = work.tile([P, PATTERNS], F32, name="log_signal", bufs=8)
            for i in range(pieces):
                n = slice(i * PATTERNS // pieces, (i + 1) * PATTERNS // pieces)
                nc.scalar.activation(out=log_signal[m][:, n], in_=signal[m][:, n], func=ACT.Ln)

        def finish(m, pieces=1):
            for i in range(pieces):
                n = slice(i * PATTERNS // pieces, (i + 1) * PATTERNS // pieces)
                result = work.tile([P, PATTERNS], F32, name="result", bufs=8)
                nc.vector.tensor_tensor(
                    out=result[:, n], in0=log_signal[m][:, n], in1=log_interference[m][:, n], op=ALU.subtract
                )
                nc.sync.dma_start(out=out[m * P : (m + 1) * P, n], in_=result[:, n])


        for g in range(GROUPS):
            reorder_gain_codes(g)
        for g in range(GROUPS):
            reorder_gain_scales(g)
        for m in (0, 1):
            for g in range(GROUPS):
                multiply_beta(m, g)
        copy_beta(0, 0)
        square_beta(0, 1)
        square_beta(0, 0)
        copy_beta(1, 0)
        copy_beta(0, 1)
        square_beta(1, 1)
        square_beta(1, 0)
        copy_beta(1, 1)
        interleave_load(0)
        interleave_load(1)
        multiply_beta(2, 0)
        multiply_beta(2, 1)
        transpose_split(0)
        transpose_split(1)
        square_beta(2, 1)
        copy_beta(2, 0)
        square_beta(2, 0)
        copy_beta(2, 1)
        copy_split(0, 0)
        copy_split(0, 1)
        quantize_beta(0)
        quantize_load()
        quantize_split(0)
        transpose_split(2)
        multiply_power(0)
        copy_split(1, 0)
        copy_split(1, 1)
        quantize_beta(1)
        quantize_split(1)

        copy_split(2, 0)
        copy_split(2, 1)
        transpose_split(3)
        quantize_beta(2)
        copy_power(0)
        multiply_power(1)
        quantize_split(2)
        quantize_power(0)

        copy_split(3, 0)
        copy_split(3, 1)
        copy_power(1)
        multiply_power(2)
        quantize_split(3)
        quantize_power(1)

        copy_power(2)
        multiply_power(3)
        quantize_power(2)

        multiply_signal(0)
        multiply_signal(1)
        for m in range(3, EARLY):
            for g in range(GROUPS):
                multiply_beta(m, g)
        copy_power(3)
        quantize_power(3)
        take_log_signal(0)
        take_log_signal(1)
        copy_beta(3, 0)
        square_beta(3, 1)
        square_beta(3, 0)
        copy_beta(4, 0)
        copy_beta(3, 1)


        for i in range(TILES):
            j = i + AHEAD
            if i == 0:
                multiply_interference(0)
                multiply_interference(1)
            elif i > 1:
                multiply_interference(i)
                multiply_signal(i)
            if EARLY <= j + 1 < TILES:
                for g in range(GROUPS):
                    multiply_beta(j + 1, g)
            beta = EARLY - 1 <= j < TILES
            if beta:
                if j >= EARLY:
                    copy_beta(j, 0)
                square_beta(j, 1)
                square_beta(j, 0)
            if EARLY - 2 <= j - 1 < TILES:
                quantize_beta(j - 1)
            if 0 <= i - 2 < DEFERRED:
                finish(i - 2)
            if beta:
                copy_beta(j, 1)
            take_log_interference(i)
            if i > 1:
                take_log_signal(i, pieces=2 if i == TILES - 1 else 1)
            if i == TILES - 2:
                for m in range(DEFERRED, TILES - 2):
                    finish(m)
        finish(TILES - 2)
        finish(TILES - 1, pieces=2)
